import numpy as np
import ml_dtypes


def mxq(x, axis, fmt="e4m3"):
    dtype, down = {"e4m3": (ml_dtypes.float8_e4m3fn, 7), "e5m2": (ml_dtypes.float8_e5m2, 14)}[fmt]
    v = np.moveaxis(np.asarray(x, np.float32).astype(ml_dtypes.bfloat16).astype(np.float64), axis, -1)
    blocks = v.reshape(v.shape[:-1] + (-1, 32))
    amax = np.abs(blocks).max(-1, keepdims=True)
    byte = np.maximum(np.where(amax > 0, np.frexp(amax)[1] - 1 + 127, 0) - down, 1)
    scale = np.exp2(byte - 127.0)
    codes = (blocks / scale).astype(np.float32).astype(dtype).astype(np.float64)
    return np.moveaxis((codes * scale).reshape(v.shape), -1, axis)


WIDE = False


def mx_kscale(k):
    if not WIDE:
        return np.ones(k)
    levels = np.array([10, -10, 5, -5, 0])
    if k % 512:
        return np.exp2(np.random.permutation(np.resize(levels, k // 32))).repeat(32)
    a = np.empty((k // 512, 16))
    for p in range(k // 512):
        a[p, :8] = np.random.permutation(np.resize(levels, 8))
        for g in range(8):
            far = levels[np.abs(levels - a[p, g]) >= 10]
            a[p, g + 8] = far[np.random.randint(len(far))]
    return np.exp2(a.ravel()).repeat(32)


BF16 = ml_dtypes.bfloat16


def bf(x):
    return np.asarray(x, np.float32).astype(BF16)


def f64(x):
    return np.asarray(x).astype(np.float64)


E2M1 = np.array([0.0, 0.5, 1.0, 1.5, 2.0, 3.0, 4.0, 6.0, -0.0, -0.5, -1.0, -1.5, -2.0, -3.0, -4.0, -6.0])


def pack_weight(w, fmt):
    k, n = w.shape
    w = f64(bf(w)).reshape(k // 32, 32, n)
    amax = np.abs(w).max(1)
    if fmt == "e4m3":
        byte = np.frexp(amax)[1] - 1 + 127 - 7
    else:
        mant, ex = np.frexp(amax / 6.0)
        byte = np.where(mant > 0.5, ex, ex - 1) + 127
    byte = np.clip(np.where(amax > 0, byte, 1), 1, 254)
    scaled = (w * np.exp2(127.0 - byte)[:, None, :]).reshape(k, n).astype(np.float32)
    by_word = np.ascontiguousarray(scaled.reshape(k // 512, 128, 4, n).transpose(0, 1, 3, 2))
    if fmt == "e4m3":
        words = by_word.astype(ml_dtypes.float8_e4m3fn).view(np.uint8)
    else:
        c = by_word.astype(ml_dtypes.float4_e2m1fn).view(np.uint8) & 0xF
        words = c[..., 0::2] | (c[..., 1::2] << 4)
    return np.ascontiguousarray(words), np.ascontiguousarray(byte.astype(np.uint8).reshape(k // 512, 16, n))


def unpack_weight(words, scales, fmt):
    g, p, n, _ = words.shape
    if fmt == "e4m3":
        vals = np.ascontiguousarray(words).view(ml_dtypes.float8_e4m3fn).astype(np.float64)
    else:
        nib = np.empty((g, p, n, 4), np.uint8)
        nib[..., 0::2] = words & 0xF
        nib[..., 1::2] = words >> 4
        vals = E2M1[nib]
    vals = vals * np.repeat(np.exp2(scales.astype(np.float64) - 127.0), 8, axis=1)[..., None]
    return vals.transpose(0, 1, 3, 2).reshape(g * 512, n)
def pack4(w):
    words, scales = pack_weight(w, "e2m1")
    return words.reshape(words.shape[0], 128, -1), scales


def unpack4(words, scales):
    return unpack_weight(words.reshape(words.shape[0], 128, -1, 2), scales, "e2m1")


T, M, K1, K2 = 512, 2048, 1024, 2048


def setup_inputs():
    s1, s2 = mx_kscale(K1), mx_kscale(K2)
    ld_bg = np.random.standard_normal((K2, M)) * 2.0 / np.sqrt(K2) / s2[:, None]
    ld_bg_words, ld_bg_scales = pack4(ld_bg)
    return {"z": bf(2.0 * np.random.standard_normal((T, M))),
            "pip_lead": bf(np.random.random((T, K1))),
            "mu_lead": bf(np.random.standard_normal((T, K1)) * s1),
            "ld_lead": bf(np.random.standard_normal((K1, M)) * 2.0 / np.sqrt(K1) / s1[:, None]),
            "pip_bg": bf(np.random.random((T, K2))),
            "mu_bg": bf(np.random.standard_normal((T, K2)) * s2),
            "ld_bg_words": ld_bg_words,
            "ld_bg_scales": ld_bg_scales,
            "inv_sd": bf(1.0 + 0.1 * np.random.standard_normal(M))}


def reference(z, pip_lead, mu_lead, ld_lead, pip_bg, mu_bg, ld_bg_words, ld_bg_scales, inv_sd):
    b_lead = f64(pip_lead) * f64(mu_lead)
    b_bg = f64(pip_bg) * f64(mu_bg)
    fit = ((mxq(b_lead, 1, "e4m3") @ mxq(f64(ld_lead), 0, "e4m3"))
           + (mxq(b_bg, 1, "e4m3") @ unpack4(ld_bg_words, ld_bg_scales)))
    return (f64(z) - fit) * f64(inv_sd)

@@ -1,0 +1,280 @@
+from contextlib import ExitStack
+import concourse.mybir as mybir
+from concourse.masks import make_identity
+
+T, M, K1, K2 = 512, 2048, 1024, 2048
+F32 = mybir.dt.float32
+BF16 = mybir.dt.bfloat16
+U8 = mybir.dt.uint8
+I32 = mybir.dt.int32
+U32 = mybir.dt.uint32
+E4 = mybir.dt.float8_e4m3fn_x4
+E2 = mybir.dt.float4_e2m1fn_x4
+ALU = mybir.AluOpType
+FLOPS = 2 * T * M * (K1 + K2)
+P = 128
+N = 512
+
+
+def tile_fine_mapping_residual_s1_kernel(tc, z, pip_lead, mu_lead, ld_lead, pip_bg, mu_bg, ld_words, ld_scales, inv_sd, out):
+    nc = tc.nc
+    with ExitStack() as ctx:
+        keep = ctx.enter_context(tc.tile_pool(name="keep", bufs=1))
+        work = ctx.enter_context(tc.tile_pool(name="work", bufs=2))
+        psum = ctx.enter_context(tc.psum_pool(name="psum", bufs=1))
+
+        pbv = pip_bg.rearrange("(p r) k -> p r k", r=4)
+        mbv = mu_bg.rearrange("(p r) k -> p r k", r=4)
+        plv = pip_lead.rearrange("(p r) k -> p r k", r=4)
+        mlv = mu_lead.rearrange("(p r) k -> p r k", r=4)
+        zv = z.rearrange("(p r) m -> p r m", r=4)
+        ov = out.rearrange("(p r) m -> p r m", r=4)
+        ldv = ld_lead.rearrange("(g p j) m -> g p j m", p=P, j=4)
+        wv = ld_words.bitcast(I32).rearrange("g p b -> p g b")
+        sv = ld_scales.bitcast(I32).rearrange("g q n -> q g n")
+
+        ident = keep.tile([P, P], F32, name="ident")
+        identb = keep.tile([P, P], BF16, name="identb")
+        planes = keep.tile([P, 4, M], U8, name="planes", align_bytes=64)
+        words = keep.tile([P, 4, 2 * M], U8, name="words", align_bytes=64)
+        ldc = keep.tile([P, 2, M], U32, name="ldc", align_bytes=64)
+        lds = keep.tile([P, 2, M], U8, name="lds", align_bytes=64)
+        bcod = keep.tile([P, 4, 6, P], U32, name="bcod", align_bytes=64)
+        bsc = keep.tile([P, 4, 6, P], U8, name="bsc", align_bytes=64)
+        z_sb = keep.tile([P, 4, M], BF16, name="z_sb")
+        inv_rows = keep.tile([P, P], BF16, name="inv_rows")
+        inv_cols = keep.tile([P, 16], BF16, name="inv_cols")
+        inv_bc = keep.tile([P, M], BF16, name="inv_bc")
+        pb = keep.tile([P, 4, K2], BF16, name="pb")
+        mb = keep.tile([P, 4, K2], BF16, name="mb")
+        pl = keep.tile([P, 4, K1], BF16, name="pl")
+        ml = keep.tile([P, 4, K1], BF16, name="ml")
+        ldr = {}
+        for g in range(2):
+            for h in range(2):
+                ldr[g, h] = keep.tile([P, 4, 1024], BF16, name="ldr%d%d" % (g, h))
+
+        nc.vector.memset(planes[:].rearrange("p g n -> p (g n)").bitcast(I32), 0)
+        nc.vector.memset(inv_rows[:], 0.0)
+        make_identity(nc, ident[:])
+        make_identity(nc, identb[:])
+        L = nc.sync.dma_start
+
+        def ld_b(src0, src1, dst0, dst1, r, lo, hi):
+            L(out=dst0[:, r, lo:hi], in_=src0[:, r, lo:hi])
+            L(out=dst1[:, r, lo:hi], in_=src1[:, r, lo:hi])
+
+        def ld_w(g):
+            L(out=words[:, g : g + 2, :].bitcast(I32), in_=wv[:, g : g + 2, :])
+
+        def ld_l(g, h):
+            L(out=ldr[g, h][:], in_=ldv[g][:, :, 1024 * h : 1024 * h + 1024])
+
+        def ld_z(r):
+            L(out=z_sb[:, r, :], in_=zv[:, r, :])
+
+        def ld_lead(r):
+            L(out=pl[:, r : r + 2, :], in_=plv[:, r : r + 2, :])
+            L(out=ml[:, r : r + 2, :], in_=mlv[:, r : r + 2, :])
+
+        for q in range(4):
+            nc.gpsimd.dma_start(out=planes[32 * q : 32 * q + 4, :, :].bitcast(I32), in_=sv[4 * q : 4 * q + 4, :, :])
+        nc.gpsimd.dma_start(out=inv_rows[0:16, :], in_=inv_sd.rearrange("(c p) -> c p", p=P))
+
+        ld_b(pbv, mbv, pb, mb, 0, 0, 1024); ld_b(pbv, mbv, pb, mb, 0, 1024, 2048)
+        ld_w(0)
+        ld_w(2)
+        ld_l(0, 0)
+        ld_b(pbv, mbv, pb, mb, 1, 0, 2048)
+        ld_lead(0)
+        ld_l(1, 0)
+        ld_z(0)
+        ld_l(0, 1)
+        ld_z(1)
+        ld_l(1, 1)
+        ld_b(pbv, mbv, pb, mb, 2, 0, 2048)
+        ld_lead(2)
+        ld_z(2)
+        ld_b(pbv, mbv, pb, mb, 3, 0, 2048)
+        ld_z(3)
+
+        prod = {}
+        xps = {}
+        grp = {}
+
+        def M_(r, c):
+            x = work.tile([P, 1024], BF16, name="prod", bufs=4)
+            a, b = (pb, mb) if c < 2 else (pl, ml)
+            o = 1024 * c if c < 2 else 0
+            x = x[:].rearrange("p (u w e) -> p u w e", u=2, e=2)
+            nc.vector.tensor_mul(
+                out=x,
+                in0=a[:, r, o : o + 1024].rearrange("p (w u e) -> p u w e", u=2, e=2),
+                in1=b[:, r, o : o + 1024].rearrange("p (w u e) -> p u w e", u=2, e=2),
+            )
+            prod[r, c] = x
+
+        def T_(r, c):
+            xp = psum.tile([P, 4, P], F32, name="xp", bufs=2)
+            w = prod[r, c].rearrange("p u w e -> p (u w e)").bitcast(F32)
+            for g in range(2):
+                for u in range(2):
+                    nc.tensor.transpose(xp[:, 2 * g + u, :], w[:, 256 * u + 128 * g : 256 * u + 128 * g + 128], ident[:])
+            xps[r, c] = xp
+
+        def C_(r, c, eng="A"):
+            x = work.tile([P, 2, P, 4], BF16, name="grp", bufs=4, align_bytes=64)
+            o = x[:].bitcast(F32)
+            i = xps[r, c][:].rearrange("p (g u) t -> p g t u", u=2)
+            if eng == "A":
+                nc.scalar.copy(out=o, in_=i)
+            else:
+                nc.vector.tensor_copy(out=o, in_=i)
+            grp[r, c] = x
+
+        def Q_(r, c):
+            nc.vector.quantize_mx(
+                out=bcod[:, r, 2 * c : 2 * c + 2, :].rearrange("p g t -> p (g t)").bitcast(E4),
+                scales=bsc[:, r, 2 * c : 2 * c + 2, :].rearrange("p g t -> p (g t)"),
+                in_=grp[r, c][:].rearrange("p g t j -> p (g t j)"),
+            )
+
+        lg = {}
+
+        def I_(g, n, split=0):
+            x = work.tile([P, N, 4], BF16, name="lg", bufs=3, align_bytes=64)
+            raw = ldr[g, n // 2]
+            for eng, lo, hi in (("V", 0, split), ("A", split, N)):
+                if hi == lo:
+                    continue
+                o = x[:, lo:hi, :].rearrange("p (c i) j -> p c j i", i=4)
+                b = 512 * (n % 2)
+                i = raw[:, :, b + lo : b + hi].rearrange("p j (c i) -> p c j i", i=4)
+                if eng == "A":
+                    nc.scalar.copy(out=o, in_=i)
+                else:
+                    nc.vector.tensor_copy(out=o, in_=i)
+            lg[g, n] = x
+
+        def QL(g, n):
+            nc.vector.quantize_mx(
+                out=ldc[:, g, N * n : N * n + N].bitcast(E4),
+                scales=lds[:, g, N * n : N * n + N],
+                in_=lg[g, n][:].rearrange("p n j -> p (n j)"),
+            )
+
+        acc = {}
+        cnt = {}
+
+        def MM(r, n, passes):
+            if (r, n) not in acc:
+                acc[r, n] = psum.tile([P, N], F32, name="acc", bufs=6)
+                cnt[r, n] = 0
+            for k in passes:
+                if k < 4:
+                    rhs = words[:, k, 2 * N * n : 2 * N * n + 2 * N].bitcast(E2)
+                    rs = planes[:, k, N * n : N * n + N]
+                else:
+                    rhs = ldc[:, k - 4, N * n : N * n + N].bitcast(E4)
+                    rs = lds[:, k - 4, N * n : N * n + N]
+                nc.tensor.matmul_mx(
+                    out=acc[r, n][:],
+                    lhsT=bcod[:, r, k, :].bitcast(E4),
+                    lhsT_scale=bsc[:, r, k, :],
+                    rhs=rhs,
+                    rhs_scale=rs,
+                    start=cnt[r, n] == 0,
+                    stop=cnt[r, n] == 5,
+                )
+                cnt[r, n] += 1
+
+        res = {}
+        dif = {}
+
+        def A_(r, n):
+            d = work.tile([P, N], F32, name="dif", bufs=4)
+            nc.vector.tensor_sub(out=d[:], in0=z_sb[:, r, N * n : N * n + N], in1=acc[r, n][:])
+            dif[r, n] = d
+
+        def E_(r, n, eng="V"):
+            if (r, n // 2) not in res:
+                res[r, n // 2] = work.tile([P, 2, N], F32, name="res", bufs=4)
+            e = nc.vector if eng == "V" else nc.gpsimd
+            e.tensor_mul(out=res[r, n // 2][:, n % 2, :], in0=dif[r, n][:], in1=inv_bc[:, N * n : N * n + N])
+
+        def S_(r, h):
+            L(out=ov[:, r, 1024 * h : 1024 * h + 1024].rearrange("p (a b) -> p a b", a=2), in_=res[r, h][:])
+
+        def S1(r, n):
+            L(out=ov[:, r, N * n : N * n + N], in_=res[r, n // 2][:, n % 2, :])
+
+        def INV():
+            ip = psum.tile([P, P], BF16, name="xp", bufs=2)
+            nc.tensor.transpose(ip[:], inv_rows[:], identb[:])
+            nc.scalar.copy(out=inv_cols[:], in_=ip[:, 0:16])
+            for b in range(2):
+                ib = psum.tile([P, 8, P], BF16, name="xp", bufs=2)
+                for c in range(8):
+                    nc.tensor.transpose(ib[:, c, :], inv_cols[:, 8 * b + c : 8 * b + c + 1].to_broadcast([P, P]), identb[:])
+                nc.scalar.copy(out=inv_bc[:, 1024 * b : 1024 * b + 1024], in_=ib[:].rearrange("p c t -> p (c t)"))
+
+        def prep(r, c, eng="A"):
+            M_(r, c)
+            T_(r, c)
+            C_(r, c, eng)
+            Q_(r, c)
+
+
+        def lead(g, n, split):
+            I_(g, n, split)
+            QL(g, n)
+
+
+        def tile(r, n):
+            MM(r, n, [0, 1, 2, 3, 4, 5])
+
+
+        def epi(r, n, eng="V"):
+            A_(r, n)
+            E_(r, n, eng)
+            if n % 2:
+                S_(r, n // 2)
+
+
+        prep(0, 0)
+        prep(0, 1)
+        lead(0, 0, 256)
+        lead(0, 1, 256)
+        INV()
+        prep(0, 2)
+        lead(1, 0, 256)
+        lead(1, 1, 256)
+        MM(0, 0, range(6))
+        MM(0, 1, range(6))
+        prep(1, 0)
+        prep(1, 1)
+        prep(1, 2)
+        MM(1, 0, range(6))
+        MM(1, 1, range(6))
+        epi(0, 0)
+        epi(0, 1)
+        lead(0, 2, 0)
+        lead(0, 3, 0)
+        epi(1, 0)
+        epi(1, 1)
+        lead(1, 2, 0)
+        lead(1, 3, 0)
+        MM(0, 2, range(6))
+        MM(0, 3, range(6))
+        for c in range(3): prep(2, c)
+        MM(1, 2, range(6))
+        MM(1, 3, range(6))
+        epi(0, 2)
+        epi(0, 3)
+        for c in range(3): prep(3, 2 - c)
+        for r, n in ((2, 0), (2, 1), (2, 2), (2, 3), (3, 0), (3, 1), (3, 2), (3, 3)):
+            MM(r, n, range(6))
+        epi(1, 2)
+        epi(1, 3)
+        for r, n in ((2, 0), (2, 1), (2, 2), (2, 3), (3, 0), (3, 1), (3, 2), (3, 3)):
+            epi(r, n)

@@ -23,6 +23,7 @@ def tile_fine_mapping_residual_s1_kernel(tc, z, pip_lead, mu_lead, ld_lead, pip_
         work = ctx.enter_context(tc.tile_pool(name="work", bufs=2))
         psum = ctx.enter_context(tc.psum_pool(name="psum", bufs=1))
 
+        ctx.enter_context(tc.manual_schedule())
         pbv = pip_bg.rearrange("(p r) k -> p r k", r=4)
         mbv = mu_bg.rearrange("(p r) k -> p r k", r=4)
         plv = pip_lead.rearrange("(p r) k -> p r k", r=4)
@@ -36,7 +37,7 @@ def tile_fine_mapping_residual_s1_kernel(tc, z, pip_lead, mu_lead, ld_lead, pip_
         ident = keep.tile([P, P], F32, name="ident")
         identb = keep.tile([P, P], BF16, name="identb")
         planes = keep.tile([P, 4, M], U8, name="planes", align_bytes=64)
-        words = keep.tile([P, 4, 2 * M], U8, name="words", align_bytes=64)
+        words = [keep.tile([P, 4, M], U8, name="words%d" % h, align_bytes=64) for h in range(2)]
         ldc = keep.tile([P, 2, M], U32, name="ldc", align_bytes=64)
         lds = keep.tile([P, 2, M], U8, name="lds", align_bytes=64)
         bcod = keep.tile([P, 4, 6, P], U32, name="bcod", align_bytes=64)
@@ -64,8 +65,8 @@ def tile_fine_mapping_residual_s1_kernel(tc, z, pip_lead, mu_lead, ld_lead, pip_
             L(out=dst0[:, r, lo:hi], in_=src0[:, r, lo:hi])
             L(out=dst1[:, r, lo:hi], in_=src1[:, r, lo:hi])
 
-        def ld_w(g):
-            L(out=words[:, g : g + 2, :].bitcast(I32), in_=wv[:, g : g + 2, :])
+        def ld_w(h):
+            L(out=words[h][:].bitcast(I32), in_=wv[:, :, 512 * h : 512 * h + 512])
 
         def ld_l(g, h):
             L(out=ldr[g, h][:], in_=ldv[g][:, :, 1024 * h : 1024 * h + 1024])
@@ -73,29 +74,36 @@ def tile_fine_mapping_residual_s1_kernel(tc, z, pip_lead, mu_lead, ld_lead, pip_
         def ld_z(r):
             L(out=z_sb[:, r, :], in_=zv[:, r, :])
 
+        def ld_z2(r):
+            L(out=z_sb[:, r : r + 2, :], in_=zv[:, r : r + 2, :])
+
         def ld_lead(r):
             L(out=pl[:, r : r + 2, :], in_=plv[:, r : r + 2, :])
             L(out=ml[:, r : r + 2, :], in_=mlv[:, r : r + 2, :])
 
-        for q in range(4):
-            nc.gpsimd.dma_start(out=planes[32 * q : 32 * q + 4, :, :].bitcast(I32), in_=sv[4 * q : 4 * q + 4, :, :])
-        nc.gpsimd.dma_start(out=inv_rows[0:16, :], in_=inv_sd.rearrange("(c p) -> c p", p=P))
 
-        ld_b(pbv, mbv, pb, mb, 0, 0, 1024); ld_b(pbv, mbv, pb, mb, 0, 1024, 2048)
-        ld_w(0)
-        ld_w(2)
-        ld_l(0, 0)
+        def ld_s():
+            for q in range(4):
+                L(out=planes[q : P : 32, :, :].bitcast(I32), in_=sv[q : 16 : 4, :, :])
+            L(out=inv_rows[0:16, :], in_=inv_sd.rearrange("(c p) -> c p", p=P))
+
         ld_b(pbv, mbv, pb, mb, 1, 0, 2048)
-        ld_lead(0)
-        ld_l(1, 0)
-        ld_z(0)
-        ld_l(0, 1)
-        ld_z(1)
-        ld_l(1, 1)
+        ld_b(pbv, mbv, pb, mb, 0, 0, 1024)
         ld_b(pbv, mbv, pb, mb, 2, 0, 2048)
+        ld_lead(0)
+        ld_b(pbv, mbv, pb, mb, 0, 1024, 2048)
         ld_lead(2)
-        ld_z(2)
+        ld_s()
+        ld_w(0)
+        ld_l(0, 0)
+        ld_l(1, 0)
         ld_b(pbv, mbv, pb, mb, 3, 0, 2048)
+        ld_z(0)
+        ld_z(1)
+        ld_z(2)
+        ld_l(1, 1)
+        ld_w(1)
+        ld_l(0, 1)
         ld_z(3)
 
         prod = {}
@@ -103,27 +111,22 @@ def tile_fine_mapping_residual_s1_kernel(tc, z, pip_lead, mu_lead, ld_lead, pip_
         grp = {}
 
         def M_(r, c):
-            x = work.tile([P, 1024], BF16, name="prod", bufs=4)
+            x = work.tile([P, 1024], BF16, name="prod", bufs=6)
             a, b = (pb, mb) if c < 2 else (pl, ml)
             o = 1024 * c if c < 2 else 0
-            x = x[:].rearrange("p (u w e) -> p u w e", u=2, e=2)
-            nc.vector.tensor_mul(
-                out=x,
-                in0=a[:, r, o : o + 1024].rearrange("p (w u e) -> p u w e", u=2, e=2),
-                in1=b[:, r, o : o + 1024].rearrange("p (w u e) -> p u w e", u=2, e=2),
-            )
+            nc.vector.tensor_mul(out=x[:], in0=a[:, r, o : o + 1024], in1=b[:, r, o : o + 1024])
             prod[r, c] = x
 
         def T_(r, c):
             xp = psum.tile([P, 4, P], F32, name="xp", bufs=2)
-            w = prod[r, c].rearrange("p u w e -> p (u w e)").bitcast(F32)
+            w = prod[r, c][:].bitcast(F32)
             for g in range(2):
                 for u in range(2):
-                    nc.tensor.transpose(xp[:, 2 * g + u, :], w[:, 256 * u + 128 * g : 256 * u + 128 * g + 128], ident[:])
+                    nc.tensor.transpose(xp[:, 2 * g + u, :], w[:, 256 * g + u : 256 * (g + 1) : 2], ident[:])
             xps[r, c] = xp
 
         def C_(r, c, eng="A"):
-            x = work.tile([P, 2, P, 4], BF16, name="grp", bufs=4, align_bytes=64)
+            x = work.tile([P, 2, P, 4], BF16, name="grp", bufs=6, align_bytes=64)
             o = x[:].bitcast(F32)
             i = xps[r, c][:].rearrange("p (g u) t -> p g t u", u=2)
             if eng == "A":
@@ -172,7 +175,7 @@ def tile_fine_mapping_residual_s1_kernel(tc, z, pip_lead, mu_lead, ld_lead, pip_
                 cnt[r, n] = 0
             for k in passes:
                 if k < 4:
-                    rhs = words[:, k, 2 * N * n : 2 * N * n + 2 * N].bitcast(E2)
+                    rhs = words[n // 2][:, k, 2 * N * (n % 2) : 2 * N * (n % 2) + 2 * N].bitcast(E2)
                     rs = planes[:, k, N * n : N * n + N]
                 else:
                     rhs = ldc[:, k - 4, N * n : N * n + N].bitcast(E4)
@@ -192,13 +195,13 @@ def tile_fine_mapping_residual_s1_kernel(tc, z, pip_lead, mu_lead, ld_lead, pip_
         dif = {}
 
         def A_(r, n):
-            d = work.tile([P, N], F32, name="dif", bufs=4)
+            d = work.tile([P, N], F32, name="dif", bufs=6)
             nc.vector.tensor_sub(out=d[:], in0=z_sb[:, r, N * n : N * n + N], in1=acc[r, n][:])
             dif[r, n] = d
 
         def E_(r, n, eng="V"):
             if (r, n // 2) not in res:
-                res[r, n // 2] = work.tile([P, 2, N], F32, name="res", bufs=4)
+                res[r, n // 2] = work.tile([P, 2, N], F32, name="res", bufs=6)
             e = nc.vector if eng == "V" else nc.gpsimd
             e.tensor_mul(out=res[r, n // 2][:, n % 2, :], in0=dif[r, n][:], in1=inv_bc[:, N * n : N * n + N])
 
@@ -218,63 +221,24 @@ def tile_fine_mapping_residual_s1_kernel(tc, z, pip_lead, mu_lead, ld_lead, pip_
                     nc.tensor.transpose(ib[:, c, :], inv_cols[:, 8 * b + c : 8 * b + c + 1].to_broadcast([P, P]), identb[:])
                 nc.scalar.copy(out=inv_bc[:, 1024 * b : 1024 * b + 1024], in_=ib[:].rearrange("p c t -> p (c t)"))
 
-        def prep(r, c, eng="A"):
-            M_(r, c)
-            T_(r, c)
-            C_(r, c, eng)
-            Q_(r, c)
-
-
-        def lead(g, n, split):
-            I_(g, n, split)
-            QL(g, n)
-
-
-        def tile(r, n):
-            MM(r, n, [0, 1, 2, 3, 4, 5])
-
-
-        def epi(r, n, eng="V"):
-            A_(r, n)
-            E_(r, n, eng)
-            if n % 2:
-                S_(r, n // 2)
-
-
-        prep(0, 0)
-        prep(0, 1)
-        lead(0, 0, 256)
-        lead(0, 1, 256)
-        INV()
-        prep(0, 2)
-        lead(1, 0, 256)
-        lead(1, 1, 256)
-        MM(0, 0, range(6))
-        MM(0, 1, range(6))
-        prep(1, 0)
-        prep(1, 1)
-        prep(1, 2)
-        MM(1, 0, range(6))
-        MM(1, 1, range(6))
-        epi(0, 0)
-        epi(0, 1)
-        lead(0, 2, 0)
-        lead(0, 3, 0)
-        epi(1, 0)
-        epi(1, 1)
-        lead(1, 2, 0)
-        lead(1, 3, 0)
-        MM(0, 2, range(6))
-        MM(0, 3, range(6))
-        for c in range(3): prep(2, c)
-        MM(1, 2, range(6))
-        MM(1, 3, range(6))
-        epi(0, 2)
-        epi(0, 3)
-        for c in range(3): prep(3, 2 - c)
-        for r, n in ((2, 0), (2, 1), (2, 2), (2, 3), (3, 0), (3, 1), (3, 2), (3, 3)):
-            MM(r, n, range(6))
-        epi(1, 2)
-        epi(1, 3)
-        for r, n in ((2, 0), (2, 1), (2, 2), (2, 3), (3, 0), (3, 1), (3, 2), (3, 3)):
-            epi(r, n)
+        M_(2, 0); M_(1, 2); M_(2, 1); T_(2, 1); C_(2, 1); M_(0, 0); T_(0, 0); C_(0, 0)
+        M_(0, 1); M_(1, 0); T_(2, 0); C_(2, 0); Q_(0, 0); T_(1, 2); C_(1, 2); M_(1, 1)
+        T_(0, 1); C_(0, 1); M_(2, 2); T_(1, 0); C_(1, 0); Q_(2, 1); M_(3, 2); M_(0, 2)
+        Q_(0, 1); T_(3, 2); C_(3, 2); Q_(2, 0); Q_(1, 0); T_(2, 2); C_(2, 2); T_(1, 1); C_(1, 1)
+        Q_(1, 2); Q_(3, 2); Q_(1, 1); INV(); I_(0, 1, 256); MM(0, 0, range(4))
+        Q_(2, 2); I_(0, 0, 384); QL(0, 1); MM(2, 0, range(4)); I_(1, 0, 256); T_(0, 2); C_(0, 2)
+        QL(0, 0); QL(1, 0); I_(1, 1, 256); MM(0, 1, range(4)); MM(2, 1, range(4)); M_(3, 1)
+        Q_(0, 2); MM(1, 0, range(4)); MM(2, 0, (4, 5)); MM(1, 1, range(4)); QL(1, 1); MM(0, 0, (4, 5))
+        MM(1, 1, (4, 5)); M_(3, 0); T_(3, 0); C_(3, 0); A_(0, 0); T_(3, 1); C_(3, 1); MM(2, 1, (4, 5))
+        E_(0, 0, "V"); Q_(3, 0); MM(0, 1, (4, 5)); A_(2, 1); MM(1, 0, (4, 5)); Q_(3, 1)
+        A_(2, 0); A_(0, 1); MM(3, 0, range(4)); I_(1, 2, 256); MM(3, 0, (4, 5)); E_(2, 0, "V")
+        E_(0, 1, "V"); A_(1, 0); MM(3, 1, (4, 5)); A_(1, 1); E_(2, 1, "G"); MM(3, 1, range(4))
+        QL(1, 2); MM(0, 3, range(4)); E_(1, 0, "V"); I_(1, 3, 0); QL(1, 3); S_(0, 0)
+        I_(0, 2, 384); S_(2, 0); QL(0, 2); I_(0, 3, 0); MM(0, 2, range(4)); MM(1, 2, range(4))
+        A_(3, 0); E_(1, 1, "G"); MM(1, 3, range(4)); A_(3, 1); E_(3, 0, "V"); MM(0, 2, (4, 5))
+        MM(1, 2, (4, 5)); MM(2, 2, (4, 5)); MM(2, 2, range(4)); QL(0, 3); S_(1, 0); E_(3, 1, "G")
+        MM(0, 3, (4, 5)); S_(3, 0); A_(0, 2); A_(1, 2); MM(1, 3, (4, 5)); MM(2, 3, range(4))
+        E_(0, 2, "G"); A_(0, 3); A_(1, 3); E_(0, 3, "V"); MM(2, 3, (4, 5)); S_(0, 1)
+        MM(3, 2, range(4)); E_(1, 3, "V"); MM(3, 2, (4, 5)); MM(3, 3, range(4)); A_(2, 2); E_(1, 2, "G")
+        A_(2, 3); E_(2, 2, "V"); E_(2, 3, "V"); MM(3, 3, (4, 5)); A_(3, 2); A_(3, 3)
+        E_(3, 2, "G"); S_(1, 1); S_(2, 1); E_(3, 3, "V"); S1(3, 2); S1(3, 3)

@@ -87,23 +87,23 @@ def tile_fine_mapping_residual_s1_kernel(tc, z, pip_lead, mu_lead, ld_lead, pip_
                 L(out=planes[q : P : 32, :, :].bitcast(I32), in_=sv[q : 16 : 4, :, :])
             L(out=inv_rows[0:16, :], in_=inv_sd.rearrange("(c p) -> c p", p=P))
 
-        ld_b(pbv, mbv, pb, mb, 1, 0, 2048)
         ld_b(pbv, mbv, pb, mb, 0, 0, 1024)
-        ld_b(pbv, mbv, pb, mb, 2, 0, 2048)
-        ld_lead(0)
         ld_b(pbv, mbv, pb, mb, 0, 1024, 2048)
-        ld_lead(2)
         ld_s()
+        ld_b(pbv, mbv, pb, mb, 1, 0, 2048)
+        ld_lead(0)
+        ld_b(pbv, mbv, pb, mb, 3, 0, 2048)
+        ld_b(pbv, mbv, pb, mb, 2, 0, 2048)
         ld_w(0)
         ld_l(0, 0)
         ld_l(1, 0)
-        ld_b(pbv, mbv, pb, mb, 3, 0, 2048)
-        ld_z(0)
+        ld_lead(2)
         ld_z(1)
-        ld_z(2)
-        ld_l(1, 1)
-        ld_w(1)
+        ld_z(0)
         ld_l(0, 1)
+        ld_l(1, 1)
+        ld_z(2)
+        ld_w(1)
         ld_z(3)
 
         prod = {}
@@ -221,24 +221,24 @@ def tile_fine_mapping_residual_s1_kernel(tc, z, pip_lead, mu_lead, ld_lead, pip_
                     nc.tensor.transpose(ib[:, c, :], inv_cols[:, 8 * b + c : 8 * b + c + 1].to_broadcast([P, P]), identb[:])
                 nc.scalar.copy(out=inv_bc[:, 1024 * b : 1024 * b + 1024], in_=ib[:].rearrange("p c t -> p (c t)"))
 
-        M_(2, 0); M_(1, 2); M_(2, 1); T_(2, 1); C_(2, 1); M_(0, 0); T_(0, 0); C_(0, 0)
-        M_(0, 1); M_(1, 0); T_(2, 0); C_(2, 0); Q_(0, 0); T_(1, 2); C_(1, 2); M_(1, 1)
-        T_(0, 1); C_(0, 1); M_(2, 2); T_(1, 0); C_(1, 0); Q_(2, 1); M_(3, 2); M_(0, 2)
-        Q_(0, 1); T_(3, 2); C_(3, 2); Q_(2, 0); Q_(1, 0); T_(2, 2); C_(2, 2); T_(1, 1); C_(1, 1)
-        Q_(1, 2); Q_(3, 2); Q_(1, 1); INV(); I_(0, 1, 256); MM(0, 0, range(4))
-        Q_(2, 2); I_(0, 0, 384); QL(0, 1); MM(2, 0, range(4)); I_(1, 0, 256); T_(0, 2); C_(0, 2)
-        QL(0, 0); QL(1, 0); I_(1, 1, 256); MM(0, 1, range(4)); MM(2, 1, range(4)); M_(3, 1)
-        Q_(0, 2); MM(1, 0, range(4)); MM(2, 0, (4, 5)); MM(1, 1, range(4)); QL(1, 1); MM(0, 0, (4, 5))
-        MM(1, 1, (4, 5)); M_(3, 0); T_(3, 0); C_(3, 0); A_(0, 0); T_(3, 1); C_(3, 1); MM(2, 1, (4, 5))
-        E_(0, 0, "V"); Q_(3, 0); MM(0, 1, (4, 5)); A_(2, 1); MM(1, 0, (4, 5)); Q_(3, 1)
-        A_(2, 0); A_(0, 1); MM(3, 0, range(4)); I_(1, 2, 256); MM(3, 0, (4, 5)); E_(2, 0, "V")
-        E_(0, 1, "V"); A_(1, 0); MM(3, 1, (4, 5)); A_(1, 1); E_(2, 1, "G"); MM(3, 1, range(4))
-        QL(1, 2); MM(0, 3, range(4)); E_(1, 0, "V"); I_(1, 3, 0); QL(1, 3); S_(0, 0)
-        I_(0, 2, 384); S_(2, 0); QL(0, 2); I_(0, 3, 0); MM(0, 2, range(4)); MM(1, 2, range(4))
-        A_(3, 0); E_(1, 1, "G"); MM(1, 3, range(4)); A_(3, 1); E_(3, 0, "V"); MM(0, 2, (4, 5))
-        MM(1, 2, (4, 5)); MM(2, 2, (4, 5)); MM(2, 2, range(4)); QL(0, 3); S_(1, 0); E_(3, 1, "G")
-        MM(0, 3, (4, 5)); S_(3, 0); A_(0, 2); A_(1, 2); MM(1, 3, (4, 5)); MM(2, 3, range(4))
-        E_(0, 2, "G"); A_(0, 3); A_(1, 3); E_(0, 3, "V"); MM(2, 3, (4, 5)); S_(0, 1)
-        MM(3, 2, range(4)); E_(1, 3, "V"); MM(3, 2, (4, 5)); MM(3, 3, range(4)); A_(2, 2); E_(1, 2, "G")
-        A_(2, 3); E_(2, 2, "V"); E_(2, 3, "V"); MM(3, 3, (4, 5)); A_(3, 2); A_(3, 3)
-        E_(3, 2, "G"); S_(1, 1); S_(2, 1); E_(3, 3, "V"); S1(3, 2); S1(3, 3)
+        M_(0, 0); M_(0, 1); M_(1, 0); T_(0, 0); C_(0, 0); M_(1, 1); M_(0, 2)
+        INV(); M_(3, 0); T_(0, 2); C_(0, 2); T_(0, 1); C_(0, 1); T_(1, 1); C_(1, 1); T_(1, 0); C_(1, 0)
+        Q_(0, 0); Q_(1, 1); T_(3, 0); C_(3, 0); M_(2, 0); M_(2, 1); Q_(0, 2)
+        Q_(3, 0); T_(2, 1); C_(2, 1); M_(1, 2); M_(3, 1); T_(2, 0); C_(2, 0); Q_(0, 1)
+        Q_(1, 0); Q_(2, 1); Q_(2, 0); I_(0, 0, 512); T_(3, 1); C_(3, 1); T_(1, 2); C_(1, 2)
+        Q_(1, 2); MM(1, 1, range(4)); QL(0, 0); I_(0, 1, 128); MM(0, 0, range(4)); I_(1, 0, 128)
+        QL(0, 1); I_(1, 1, 256); MM(0, 1, range(4)); MM(1, 0, range(4)); QL(1, 0); MM(2, 1, range(4))
+        MM(1, 0, (4, 5)); MM(0, 0, (4, 5)); M_(2, 2); M_(3, 2); QL(1, 1); T_(2, 2); C_(2, 2)
+        MM(1, 1, (4, 5)); A_(1, 0); Q_(2, 2); T_(3, 2); C_(3, 2); MM(0, 1, (4, 5)); MM(2, 0, range(4))
+        MM(2, 0, (4, 5)); A_(0, 0); I_(0, 2, 0); MM(2, 1, (4, 5)); A_(1, 1); A_(0, 1)
+        Q_(3, 1); E_(1, 0, "V"); Q_(3, 2); E_(0, 1, "V"); E_(0, 0, "V"); E_(1, 1, "V")
+        I_(1, 2, 256); MM(3, 0, (4, 5)); MM(3, 0, range(4)); MM(3, 1, range(4)); MM(3, 1, (4, 5)); QL(0, 2)
+        I_(0, 3, 0); QL(1, 2); MM(0, 2, (4, 5)); I_(1, 3, 0); MM(1, 2, (4, 5)); A_(2, 1)
+        A_(2, 0); S_(1, 0); E_(2, 1, "V"); E_(2, 0, "V"); MM(2, 2, (4, 5)); QL(0, 3)
+        A_(3, 0); MM(0, 2, range(4)); A_(0, 2); A_(3, 1); MM(1, 2, range(4)); MM(1, 3, range(4))
+        QL(1, 3); A_(1, 2); E_(3, 0, "V"); MM(1, 3, (4, 5)); MM(2, 2, range(4)); A_(1, 3)
+        MM(0, 3, (4, 5)); MM(0, 3, range(4)); MM(2, 3, (4, 5)); A_(2, 2); S_(0, 0); S_(2, 0)
+        MM(3, 2, (4, 5)); E_(3, 1, "V"); MM(2, 3, range(4)); MM(3, 2, range(4)); E_(1, 3, "V"); E_(1, 2, "V")
+        A_(0, 3); MM(3, 3, (4, 5)); E_(0, 2, "V"); E_(0, 3, "V"); MM(3, 3, range(4)); S_(1, 1)
+        A_(2, 3); S_(3, 0); S_(0, 1); E_(2, 2, "V"); A_(3, 2); E_(2, 3, "V")
+        S_(2, 1); E_(3, 2, "V"); A_(3, 3); E_(3, 3, "V"); S1(3, 2); S1(3, 3)

from contextlib import ExitStack
import concourse.mybir as mybir
from concourse.masks import make_identity

T, M, K1, K2 = 512, 2048, 1024, 2048
F32 = mybir.dt.float32
BF16 = mybir.dt.bfloat16
U8 = mybir.dt.uint8
I32 = mybir.dt.int32
U32 = mybir.dt.uint32
E4 = mybir.dt.float8_e4m3fn_x4
E2 = mybir.dt.float4_e2m1fn_x4
ALU = mybir.AluOpType
FLOPS = 2 * T * M * (K1 + K2)
P = 128
N = 512


def tile_fine_mapping_residual_s1_kernel(tc, z, pip_lead, mu_lead, ld_lead, pip_bg, mu_bg, ld_words, ld_scales, inv_sd, out):
    nc = tc.nc
    with ExitStack() as ctx:
        keep = ctx.enter_context(tc.tile_pool(name="keep", bufs=1))
        work = ctx.enter_context(tc.tile_pool(name="work", bufs=2))
        psum = ctx.enter_context(tc.psum_pool(name="psum", bufs=1))

        ctx.enter_context(tc.manual_schedule())
        pbv = pip_bg.rearrange("(p r) k -> p r k", r=4)
        mbv = mu_bg.rearrange("(p r) k -> p r k", r=4)
        plv = pip_lead.rearrange("(p r) k -> p r k", r=4)
        mlv = mu_lead.rearrange("(p r) k -> p r k", r=4)
        zv = z.rearrange("(p r) m -> p r m", r=4)
        ov = out.rearrange("(p r) m -> p r m", r=4)
        ldv = ld_lead.rearrange("(g p j) m -> g p j m", p=P, j=4)
        wv = ld_words.bitcast(I32).rearrange("g p b -> p g b")
        sv = ld_scales.bitcast(I32).rearrange("g q n -> q g n")

        ident = keep.tile([P, P], F32, name="ident")
        identb = keep.tile([P, P], BF16, name="identb")
        planes = keep.tile([P, 4, M], U8, name="planes", align_bytes=64)
        words = [keep.tile([P, 4, M], U8, name="words%d" % h, align_bytes=64) for h in range(2)]
        ldc = keep.tile([P, 2, M], U32, name="ldc", align_bytes=64)
        lds = keep.tile([P, 2, M], U8, name="lds", align_bytes=64)
        bcod = keep.tile([P, 4, 6, P], U32, name="bcod", align_bytes=64)
        bsc = keep.tile([P, 4, 6, P], U8, name="bsc", align_bytes=64)
        z_sb = keep.tile([P, 4, M], BF16, name="z_sb")
        inv_rows = keep.tile([P, P], BF16, name="inv_rows")
        inv_cols = keep.tile([P, 16], BF16, name="inv_cols")
        inv_bc = keep.tile([P, M], BF16, name="inv_bc")
        pb = keep.tile([P, 4, K2], BF16, name="pb")
        mb = keep.tile([P, 4, K2], BF16, name="mb")
        pl = keep.tile([P, 4, K1], BF16, name="pl")
        ml = keep.tile([P, 4, K1], BF16, name="ml")
        ldr = {}
        for g in range(2):
            for h in range(2):
                ldr[g, h] = keep.tile([P, 4, 1024], BF16, name="ldr%d%d" % (g, h))

        nc.vector.memset(planes[:].rearrange("p g n -> p (g n)").bitcast(I32), 0)
        nc.vector.memset(inv_rows[:], 0.0)
        make_identity(nc, ident[:])
        make_identity(nc, identb[:])
        L = nc.sync.dma_start

        def ld_b(src0, src1, dst0, dst1, r, lo, hi):
            L(out=dst0[:, r, lo:hi], in_=src0[:, r, lo:hi])
            L(out=dst1[:, r, lo:hi], in_=src1[:, r, lo:hi])

        def ld_w(h):
            L(out=words[h][:].bitcast(I32), in_=wv[:, :, 512 * h : 512 * h + 512])

        def ld_l(g, h):
            L(out=ldr[g, h][:], in_=ldv[g][:, :, 1024 * h : 1024 * h + 1024])

        def ld_z(r):
            L(out=z_sb[:, r, :], in_=zv[:, r, :])

        def ld_z2(r):
            L(out=z_sb[:, r : r + 2, :], in_=zv[:, r : r + 2, :])

        def ld_lead(r):
            L(out=pl[:, r : r + 2, :], in_=plv[:, r : r + 2, :])
            L(out=ml[:, r : r + 2, :], in_=mlv[:, r : r + 2, :])


        def ld_s():
            for q in range(4):
                L(out=planes[q : P : 32, :, :].bitcast(I32), in_=sv[q : 16 : 4, :, :])
            L(out=inv_rows[0:16, :], in_=inv_sd.rearrange("(c p) -> c p", p=P))

        ld_b(pbv, mbv, pb, mb, 0, 0, 1024)
        ld_b(pbv, mbv, pb, mb, 0, 1024, 2048)
        ld_s()
        ld_b(pbv, mbv, pb, mb, 1, 0, 2048)
        ld_lead(0)
        ld_b(pbv, mbv, pb, mb, 3, 0, 2048)
        ld_b(pbv, mbv, pb, mb, 2, 0, 2048)
        ld_w(0)
        ld_l(0, 0)
        ld_l(1, 0)
        ld_lead(2)
        ld_z(1)
        ld_z(0)
        ld_l(0, 1)
        ld_l(1, 1)
        ld_z(2)
        ld_w(1)
        ld_z(3)

        prod = {}
        xps = {}
        grp = {}

        def M_(r, c):
            x = work.tile([P, 1024], BF16, name="prod", bufs=6)
            a, b = (pb, mb) if c < 2 else (pl, ml)
            o = 1024 * c if c < 2 else 0
            nc.vector.tensor_mul(out=x[:], in0=a[:, r, o : o + 1024], in1=b[:, r, o : o + 1024])
            prod[r, c] = x

        def T_(r, c):
            xp = psum.tile([P, 4, P], F32, name="xp", bufs=2)
            w = prod[r, c][:].bitcast(F32)
            for g in range(2):
                for u in range(2):
                    nc.tensor.transpose(xp[:, 2 * g + u, :], w[:, 256 * g + u : 256 * (g + 1) : 2], ident[:])
            xps[r, c] = xp

        def C_(r, c, eng="A"):
            x = work.tile([P, 2, P, 4], BF16, name="grp", bufs=6, align_bytes=64)
            o = x[:].bitcast(F32)
            i = xps[r, c][:].rearrange("p (g u) t -> p g t u", u=2)
            if eng == "A":
                nc.scalar.copy(out=o, in_=i)
            else:
                nc.vector.tensor_copy(out=o, in_=i)
            grp[r, c] = x

        def Q_(r, c):
            nc.vector.quantize_mx(
                out=bcod[:, r, 2 * c : 2 * c + 2, :].rearrange("p g t -> p (g t)").bitcast(E4),
                scales=bsc[:, r, 2 * c : 2 * c + 2, :].rearrange("p g t -> p (g t)"),
                in_=grp[r, c][:].rearrange("p g t j -> p (g t j)"),
            )

        lg = {}

        def I_(g, n, split=0):
            x = work.tile([P, N, 4], BF16, name="lg", bufs=3, align_bytes=64)
            raw = ldr[g, n // 2]
            for eng, lo, hi in (("V", 0, split), ("A", split, N)):
                if hi == lo:
                    continue
                o = x[:, lo:hi, :].rearrange("p (c i) j -> p c j i", i=4)
                b = 512 * (n % 2)
                i = raw[:, :, b + lo : b + hi].rearrange("p j (c i) -> p c j i", i=4)
                if eng == "A":
                    nc.scalar.copy(out=o, in_=i)
                else:
                    nc.vector.tensor_copy(out=o, in_=i)
            lg[g, n] = x

        def QL(g, n):
            nc.vector.quantize_mx(
                out=ldc[:, g, N * n : N * n + N].bitcast(E4),
                scales=lds[:, g, N * n : N * n + N],
                in_=lg[g, n][:].rearrange("p n j -> p (n j)"),
            )

        acc = {}
        cnt = {}

        def MM(r, n, passes):
            if (r, n) not in acc:
                acc[r, n] = psum.tile([P, N], F32, name="acc", bufs=6)
                cnt[r, n] = 0
            for k in passes:
                if k < 4:
                    rhs = words[n // 2][:, k, 2 * N * (n % 2) : 2 * N * (n % 2) + 2 * N].bitcast(E2)
                    rs = planes[:, k, N * n : N * n + N]
                else:
                    rhs = ldc[:, k - 4, N * n : N * n + N].bitcast(E4)
                    rs = lds[:, k - 4, N * n : N * n + N]
                nc.tensor.matmul_mx(
                    out=acc[r, n][:],
                    lhsT=bcod[:, r, k, :].bitcast(E4),
                    lhsT_scale=bsc[:, r, k, :],
                    rhs=rhs,
                    rhs_scale=rs,
                    start=cnt[r, n] == 0,
                    stop=cnt[r, n] == 5,
                )
                cnt[r, n] += 1

        res = {}
        dif = {}

        def A_(r, n):
            d = work.tile([P, N], F32, name="dif", bufs=6)
            nc.vector.tensor_sub(out=d[:], in0=z_sb[:, r, N * n : N * n + N], in1=acc[r, n][:])
            dif[r, n] = d

        def E_(r, n, eng="V"):
            if (r, n // 2) not in res:
                res[r, n // 2] = work.tile([P, 2, N], F32, name="res", bufs=6)
            e = nc.vector if eng == "V" else nc.gpsimd
            e.tensor_mul(out=res[r, n // 2][:, n % 2, :], in0=dif[r, n][:], in1=inv_bc[:, N * n : N * n + N])

        def S_(r, h):
            L(out=ov[:, r, 1024 * h : 1024 * h + 1024].rearrange("p (a b) -> p a b", a=2), in_=res[r, h][:])

        def S1(r, n):
            L(out=ov[:, r, N * n : N * n + N], in_=res[r, n // 2][:, n % 2, :])

        def INV():
            ip = psum.tile([P, P], BF16, name="xp", bufs=2)
            nc.tensor.transpose(ip[:], inv_rows[:], identb[:])
            nc.scalar.copy(out=inv_cols[:], in_=ip[:, 0:16])
            for b in range(2):
                ib = psum.tile([P, 8, P], BF16, name="xp", bufs=2)
                for c in range(8):
                    nc.tensor.transpose(ib[:, c, :], inv_cols[:, 8 * b + c : 8 * b + c + 1].to_broadcast([P, P]), identb[:])
                nc.scalar.copy(out=inv_bc[:, 1024 * b : 1024 * b + 1024], in_=ib[:].rearrange("p c t -> p (c t)"))

        M_(0, 0); M_(0, 1); M_(1, 0); T_(0, 0); C_(0, 0); M_(1, 1); M_(0, 2)
        INV(); M_(3, 0); T_(0, 2); C_(0, 2); T_(0, 1); C_(0, 1); T_(1, 1); C_(1, 1); T_(1, 0); C_(1, 0)
        Q_(0, 0); Q_(1, 1); T_(3, 0); C_(3, 0); M_(2, 0); M_(2, 1); Q_(0, 2)
        Q_(3, 0); T_(2, 1); C_(2, 1); M_(1, 2); M_(3, 1); T_(2, 0); C_(2, 0); Q_(0, 1)
        Q_(1, 0); Q_(2, 1); Q_(2, 0); I_(0, 0, 512); T_(3, 1); C_(3, 1); T_(1, 2); C_(1, 2)
        Q_(1, 2); MM(1, 1, range(4)); QL(0, 0); I_(0, 1, 128); MM(0, 0, range(4)); I_(1, 0, 128)
        QL(0, 1); I_(1, 1, 256); MM(0, 1, range(4)); MM(1, 0, range(4)); QL(1, 0); MM(2, 1, range(4))
        MM(1, 0, (4, 5)); MM(0, 0, (4, 5)); M_(2, 2); M_(3, 2); QL(1, 1); T_(2, 2); C_(2, 2)
        MM(1, 1, (4, 5)); A_(1, 0); Q_(2, 2); T_(3, 2); C_(3, 2); MM(0, 1, (4, 5)); MM(2, 0, range(4))
        MM(2, 0, (4, 5)); A_(0, 0); I_(0, 2, 0); MM(2, 1, (4, 5)); A_(1, 1); A_(0, 1)
        Q_(3, 1); E_(1, 0, "V"); Q_(3, 2); E_(0, 1, "V"); E_(0, 0, "V"); E_(1, 1, "V")
        I_(1, 2, 256); MM(3, 0, (4, 5)); MM(3, 0, range(4)); MM(3, 1, range(4)); MM(3, 1, (4, 5)); QL(0, 2)
        I_(0, 3, 0); QL(1, 2); MM(0, 2, (4, 5)); I_(1, 3, 0); MM(1, 2, (4, 5)); A_(2, 1)
        A_(2, 0); S_(1, 0); E_(2, 1, "V"); E_(2, 0, "V"); MM(2, 2, (4, 5)); QL(0, 3)
        A_(3, 0); MM(0, 2, range(4)); A_(0, 2); A_(3, 1); MM(1, 2, range(4)); MM(1, 3, range(4))
        QL(1, 3); A_(1, 2); E_(3, 0, "V"); MM(1, 3, (4, 5)); MM(2, 2, range(4)); A_(1, 3)
        MM(0, 3, (4, 5)); MM(0, 3, range(4)); MM(2, 3, (4, 5)); A_(2, 2); S_(0, 0); S_(2, 0)
        MM(3, 2, (4, 5)); E_(3, 1, "V"); MM(2, 3, range(4)); MM(3, 2, range(4)); E_(1, 3, "V"); E_(1, 2, "V")
        A_(0, 3); MM(3, 3, (4, 5)); E_(0, 2, "V"); E_(0, 3, "V"); MM(3, 3, range(4)); S_(1, 1)
        A_(2, 3); S_(3, 0); S_(0, 1); E_(2, 2, "V"); A_(3, 2); E_(2, 3, "V")
        S_(2, 1); E_(3, 2, "V"); A_(3, 3); E_(3, 3, "V"); S1(3, 2); S1(3, 3)
